import numpy as np
import ml_dtypes


def mxq(x, axis, fmt="e4m3"):
    dtype, down = {"e4m3": (ml_dtypes.float8_e4m3fn, 7), "e5m2": (ml_dtypes.float8_e5m2, 14)}[fmt]
    v = np.moveaxis(np.asarray(x, np.float32).astype(ml_dtypes.bfloat16).astype(np.float64), axis, -1)
    blocks = v.reshape(v.shape[:-1] + (-1, 32))
    amax = np.abs(blocks).max(-1, keepdims=True)
    byte = np.maximum(np.where(amax > 0, np.frexp(amax)[1] - 1 + 127, 0) - down, 1)
    scale = np.exp2(byte - 127.0)
    codes = (blocks / scale).astype(np.float32).astype(dtype).astype(np.float64)
    return np.moveaxis((codes * scale).reshape(v.shape), -1, axis)


WIDE = False


def mx_kscale(k):
    if not WIDE:
        return np.ones(k)
    levels = np.array([10, -10, 5, -5, 0])
    if k % 512:
        return np.exp2(np.random.permutation(np.resize(levels, k // 32))).repeat(32)
    a = np.empty((k // 512, 16))
    for p in range(k // 512):
        a[p, :8] = np.random.permutation(np.resize(levels, 8))
        for g in range(8):
            far = levels[np.abs(levels - a[p, g]) >= 10]
            a[p, g + 8] = far[np.random.randint(len(far))]
    return np.exp2(a.ravel()).repeat(32)


def f64(x):
    return np.asarray(x).astype(np.float64)


def striped(idx):
    return np.tile(idx.reshape(-1, 16).T, (8, 1)).astype(np.uint16)


def unstriped(offs):
    return offs[:16].T.reshape(-1).astype(np.int64)


def striped8(idx):
    return np.concatenate([x.reshape(-1, 16).T for x in idx]).astype(np.uint16)


def runs(offs, k):
    lists = np.stack([offs[16 * r : 16 * r + 16].T.reshape(-1) for r in range(8)]).astype(np.int64)
    return lists[np.arange(k) % 512 // 64]


def pack_weight(w):
    k, n = w.shape
    w = f64(np.asarray(w, np.float32).astype(ml_dtypes.bfloat16)).reshape(k // 32, 32, n)
    amax = np.abs(w).max(1)
    byte = np.clip(np.where(amax > 0, np.frexp(amax)[1] - 1 + 127 - 7, 1), 1, 254)
    scaled = (w * np.exp2(127.0 - byte)[:, None, :]).reshape(k, n).astype(np.float32)
    words = np.ascontiguousarray(scaled.reshape(k // 512, 128, 4, n).transpose(0, 1, 3, 2)).astype(ml_dtypes.float8_e4m3fn).view(np.uint8)
    return words, np.ascontiguousarray(byte.astype(np.uint8).reshape(k // 512, 16, n))


def unpack_weight(words, scales):
    g, p, n, _ = words.shape
    vals = np.ascontiguousarray(words).view(ml_dtypes.float8_e4m3fn).astype(np.float64) * np.repeat(np.exp2(scales.astype(np.float64) - 127.0), 8, axis=1)[..., None]
    return vals.transpose(0, 1, 3, 2).reshape(g * 512, n)


K, T, S, G, H = 512, 1024, 512, 2048, 512


def setup_inputs():
    n = np.random.standard_normal
    s = mx_kscale(K)[:, None]
    packed_xT = pack_weight(n((K, T)) * s)
    packed_dT = pack_weight(n((K, G)) / s)
    return {
        "x_words": packed_xT[0],
        "x_scales": packed_xT[1],
        "d_words": packed_dT[0],
        "d_scales": packed_dT[1],
        "tau": np.random.uniform(0.3, 0.9, (H, 1)).astype(np.float32),
        "tau2": np.random.uniform(0.3, 0.9, (H, 1)).astype(np.float32),
        "gs": (np.random.uniform(0.5, 1.5, (K, 1)) * s).astype(np.float32),
        "tau3": np.random.uniform(0.2, 0.6, (H, 1)).astype(np.float32),
        "tau4": np.random.uniform(0.6, 1.0, (H, 1)).astype(np.float32),
        "offs": striped(np.random.permutation(T)[:S]),
        "k1": striped8(np.random.randint(0, G, (8, H))),
        "n1": striped8(np.stack([np.random.permutation(S) for _ in range(8)])),
        "n2": striped8(np.stack([np.random.permutation(S) for _ in range(8)])),
        "k2": striped8(np.random.randint(0, G, (8, H))),
        "n3": striped8(np.stack([np.random.permutation(S) for _ in range(8)])),
        "n4": striped8(np.stack([np.random.permutation(S) for _ in range(8)])),
    }


def reference(x_words, x_scales, d_words, d_scales, tau, tau2, gs, tau3, tau4, offs, k1, n1, n2, k2, n3, n4):
    d_k2 = unpack_weight(d_words, d_scales)[np.arange(K)[:, None], runs(k2, K)]
    d_k1 = unpack_weight(d_words, d_scales)[np.arange(K)[:, None], runs(k1, K)]
    xq = unpack_weight(x_words, x_scales)[:, unstriped(offs)]
    h = 0.0625 * (d_k1.T @ xq)
    top = h.max(axis=1, keepdims=True)
    ea = np.exp(f64(tau) * (h[np.arange(H)[:, None], runs(n1, H)] - top))
    ea2 = np.exp(f64(tau2) * (h[np.arange(H)[:, None], runs(n2, H)] - top))
    z = f64(gs) * (0.5 * h + np.log((ea + 0.25) / (ea2 + 0.25)))
    h2 = 0.0625 * ((d_k2.T @ mxq(z, 0, "e4m3")))
    top2 = h2.max(axis=1, keepdims=True)
    ea3 = np.exp(f64(tau3) * (h2[np.arange(H)[:, None], runs(n3, H)] - top2))
    ea4 = np.exp(f64(tau4) * (h2[np.arange(H)[:, None], runs(n4, H)] - top2))
    return 3.0 * (ea3 - ea4)

@@ -1,0 +1,206 @@
+from contextlib import ExitStack
+
+import concourse.mybir as mybir
+
+F32 = mybir.dt.float32
+BF16 = mybir.dt.bfloat16
+I32 = mybir.dt.int32
+U32 = mybir.dt.uint32
+U16 = mybir.dt.uint16
+U8 = mybir.dt.uint8
+FP8X4 = mybir.dt.float8_e4m3fn_x4
+ALU = mybir.AluOpType
+ACT = mybir.ActivationFunctionType
+
+P = 128
+PACK = 4
+K, T, S, G, H = 512, 1024, 512, 2048, 512
+HALF = S // 2
+WINDOW = 2 * S
+LIST_COLS = S // 16
+FLOPS = 2 * 2 * K * H * S
+
+
+def tile_picked_codeeosetw_none_p_kernel(
+    tc, x_words, x_scales, d_words, d_scales, tau, tau2, gs, tau3, tau4, offs, k1, n1, n2, k2, n3, n4, out
+):
+    nc = tc.nc
+    halves = [slice(0, HALF), slice(HALF, S)]
+    list_halves = [slice(0, LIST_COLS // 2), slice(LIST_COLS // 2, LIST_COLS)]
+
+    with ExitStack() as ctx:
+        keep = ctx.enter_context(tc.tile_pool(name="keep", bufs=1))
+        psum = ctx.enter_context(tc.psum_pool(name="psum", bufs=8))
+
+        def load_list(name, src):
+            tile = keep.tile([P, LIST_COLS], U16, name=name)
+            nc.sync.dma_start(tile[:], src)
+            return tile
+
+        def by_row(vec):
+            return vec.rearrange("(p t) o -> p (t o)", t=PACK)
+
+        d_bytes = keep.tile([P, G], U8, name="d_bytes", align_bytes=64)
+        x_bytes = keep.tile([P, T], U8, name="x_bytes", align_bytes=64)
+        nc.gpsimd.memset(d_bytes[:, 0 : G // 2].bitcast(I32), 0)
+        nc.vector.memset(d_bytes[:, G // 2 : G].bitcast(I32), 0)
+        nc.gpsimd.memset(x_bytes[:].bitcast(I32), 0)
+
+        k1_list = load_list("k1_list", k1)
+        offs_list = load_list("offs_list", offs)
+        nc.sync.dma_start(d_bytes[0:P:8, :].bitcast(I32), d_scales[0].bitcast(I32))
+        nc.sync.dma_start(x_bytes[0:P:8, :].bitcast(I32), x_scales[0].bitcast(I32))
+        n2_list = load_list("n2_list", n2)
+        n1_list = load_list("n1_list", n1)
+        d_table = keep.tile([P, G], I32, name="d_table", align_bytes=64)
+        nc.sync.dma_start(d_table[:], d_words[0].rearrange("p n t -> p (n t)").bitcast(I32))
+        x_table = keep.tile([P, T], I32, name="x_table", align_bytes=64)
+        nc.sync.dma_start(x_table[:], x_words[0].rearrange("p n t -> p (n t)").bitcast(I32))
+        k2_list = load_list("k2_list", k2)
+        n3_list = load_list("n3_list", n3)
+        n4_list = load_list("n4_list", n4)
+
+        windows = [keep.tile([P, WINDOW], F32, name="window%d" % t) for t in range(PACK)]
+        for t in range(PACK):
+            nc.vector.memset(windows[t][:, S:WINDOW], 0.0)
+        quarter = keep.tile([P, 1], F32, name="quarter")
+        nc.gpsimd.memset(quarter[:], 0.25)
+        rates = keep.tile([P, 4, 8], F32, name="rates")
+        gain = keep.tile([P, PACK], F32, name="gain")
+        nc.gpsimd.dma_start(rates[:, 0, 0:PACK], by_row(tau))
+        nc.gpsimd.dma_start(rates[:, 1, 0:PACK], by_row(tau2))
+        nc.gpsimd.dma_start(gain[:], by_row(gs))
+        nc.gpsimd.dma_start(rates[:, 2, 0:PACK], by_row(tau3))
+        nc.gpsimd.dma_start(rates[:, 3, 0:PACK], by_row(tau4))
+
+        def pick_scales(name, codes, tag, dealt):
+            picked = keep.tile([P, H], U8, name=name + "_picked_bytes", tag=tag, align_bytes=64)
+            nc.vector.tensor_copy(picked[:], d_bytes[:].indirect(codes[:]))
+            nc.vector.tensor_copy(
+                dealt.rearrange("p (t m) -> p t m", t=PACK), picked[:].rearrange("p (m t) -> p t m", t=PACK)
+            )
+
+        def place_scales(plane, queues):
+            for j, queue in zip(range(1, 4), queues):
+                queue.dma_start(plane[j:P:32, :].bitcast(I32), plane[8 * j : P : 32, :].bitcast(I32))
+
+        def pick_words(name, codes, tag):
+            picked = keep.tile([P, H], U32, name=name + "_picked_words", tag=tag, align_bytes=64)
+            nc.vector.tensor_copy(picked[:], d_table[:].bitcast(U32).indirect(codes[:]))
+            dealt = keep.tile([P, H], U32, name=name + "_words", align_bytes=64)
+            nc.vector.tensor_copy(
+                dealt[:].rearrange("p (t m) -> p t m", t=PACK), picked[:].rearrange("p (m t) -> p t m", t=PACK)
+            )
+            return dealt
+
+        def product(t, cols, w_words, w_bytes, a_words, a_bytes):
+            rows = slice(t * P, (t + 1) * P)
+            bank = psum.tile([P, S], F32, name="bank")
+            acc = bank[:, 0 : cols.stop - cols.start]
+            nc.tensor.matmul_mx(
+                out=acc,
+                lhsT=w_words[:, rows].bitcast(FP8X4),
+                lhsT_scale=w_bytes[:, rows],
+                rhs=a_words[:, cols].bitcast(FP8X4),
+                rhs_scale=a_bytes[:, cols],
+                start=True,
+                stop=True,
+            )
+            return acc
+
+        def layer(name, first_rate, w_words, w_bytes, a_words, a_bytes):
+            tops = keep.tile([P, PACK + 1], F32, name=name + "_tops")
+            biases = keep.tile([P, PACK, 2], F32, name=name + "_biases")
+            for t in range(PACK):
+                pieces = halves if t == 0 else [slice(0, S)]
+                so_far = None
+                for i, cols in enumerate(pieces):
+                    acc = product(t, cols, w_words, w_bytes, a_words, a_bytes)
+                    last = i == len(pieces) - 1
+                    top = tops[:, t : t + 1] if last else tops[:, PACK : PACK + 1]
+                    nc.vector.tensor_scalar(
+                        windows[t][:, cols], acc, 0.0625, so_far, ALU.mult, ALU.max, accum_out=top
+                    )
+                    so_far = top
+                nc.vector.tensor_scalar(
+                    biases[:, t, :], rates[:, first_rate : first_rate + 2, t], so_far, -1.0, ALU.mult, ALU.mult
+                )
+            return biases
+
+        def fetch_exp(dst, t, places, rate, bias):
+            nc.scalar.activation(
+                dst, windows[t][:].indirect(places), ACT.Exp, bias=bias, scale=rates[:, rate, t : t + 1]
+            )
+
+        plane1 = keep.tile([P, H + S], U8, name="plane1", tag="plane1", align_bytes=64)
+        w1_bytes, xq_bytes = plane1[:, 0:H], plane1[:, H : H + S]
+        pick_scales("w1", k1_list, "w1_picked_bytes", w1_bytes)
+        x_picked_bytes = keep.tile([P, S], U8, name="x_picked_bytes", align_bytes=64)
+        nc.vector.tensor_copy(x_picked_bytes[:], x_bytes[:].indirect(offs_list[:]))
+        nc.vector.tensor_copy(xq_bytes.bitcast(I32), x_picked_bytes[:].bitcast(I32))
+        place_scales(plane1, [nc.scalar, nc.sync, nc.scalar])
+        w1_words = pick_words("w1", k1_list, "w1_picked_words")
+        xq_words = keep.tile([P, S], U32, name="xq_words", tag="xq_words", align_bytes=64)
+        for cols, entries in zip(halves, list_halves):
+            nc.vector.tensor_copy(xq_words[:, cols], x_table[:].bitcast(U32).indirect(offs_list[:, entries]))
+
+        bias1 = layer("h", 0, w1_words, w1_bytes, xq_words, xq_bytes)
+        ea = keep.tile([P, PACK, S], F32, name="ea")
+        ea2 = keep.tile([P, PACK, S], F32, name="ea2")
+        for t in range(PACK):
+            fetch_exp(ea2[:, t, :], t, n2_list[:], 1, bias1[:, t, 1:2])
+            fetch_exp(ea[:, t, :], t, n1_list[:], 0, bias1[:, t, 0:1])
+
+        w2_bytes = keep.tile([P, H], U8, name="w2_bytes", align_bytes=64)
+        pick_scales("w2", k2_list, "plane1", w2_bytes[:])
+        place_scales(w2_bytes, [nc.sync] * 3)
+        w2_words = pick_words("w2", k2_list, "xq_words")
+        half_h = keep.tile([P, PACK, S], F32, name="half_h")
+        for t in range(PACK):
+            nc.vector.tensor_scalar(
+                half_h[:, t, :], windows[t][:, 0:S], gain[:, t : t + 1], 0.5, ALU.mult, ALU.mult
+            )
+
+        log_den = keep.tile([P, PACK, S], F32, name="log_den")
+        log_num = keep.tile([P, PACK, S], F32, name="log_num")
+        rest = keep.tile([P, PACK, S], F32, name="rest")
+        z_rows = keep.tile([P, PACK, S], BF16, name="z_rows")
+        z_packed = keep.tile([P, S, PACK], BF16, name="z_packed", align_bytes=64)
+        z_words = keep.tile([P, S], U32, name="z_words", align_bytes=64)
+        z_bytes = keep.tile([P, S], U8, name="z_bytes", align_bytes=64)
+        for t in range(PACK):
+            nc.scalar.activation(log_den[:, t, :], ea2[:, t, :], ACT.Ln, bias=quarter[:], scale=1.0)
+            nc.vector.scalar_tensor_tensor(
+                rest[:, t, :], log_den[:, t, :], gain[:, t : t + 1], half_h[:, t, :], ALU.mult, ALU.subtract
+            )
+        for cols in halves:
+            for t in range(PACK):
+                nc.scalar.activation(log_num[:, t, cols], ea[:, t, cols], ACT.Ln, bias=quarter[:], scale=1.0)
+                nc.vector.scalar_tensor_tensor(
+                    z_rows[:, t, cols], log_num[:, t, cols], gain[:, t : t + 1], rest[:, t, cols], ALU.mult, ALU.subtract
+                )
+            nc.vector.tensor_copy(
+                z_packed[:, cols, :], z_rows[:, :, cols].rearrange("p t c -> p c t")
+            )
+            nc.vector.quantize_mx(
+                out=z_words[:, cols].bitcast(FP8X4),
+                scales=z_bytes[:, cols],
+                in_=z_packed[:, cols, :].rearrange("p c t -> p (c t)"),
+            )
+
+        bias2 = layer("h2", 2, w2_words, w2_bytes, z_words, z_bytes)
+        ea3 = keep.tile([P, PACK, S], F32, name="ea3")
+        ea4 = keep.tile([P, PACK, S], F32, name="ea4")
+        triple = keep.tile([P, PACK, S], F32, name="triple")
+        result = keep.tile([P, PACK, S], F32, name="result")
+        out_rows = out.rearrange("(p t) n -> p t n", t=PACK)
+        for t in range(PACK):
+            fetch_exp(ea3[:, t, :], t, n3_list[:], 2, bias2[:, t, 0:1])
+            nc.vector.tensor_scalar(triple[:, t, :], ea3[:, t, :], 3.0, None, ALU.mult)
+            pieces = zip(halves, list_halves) if t == PACK - 1 else [(slice(0, S), slice(0, LIST_COLS))]
+            for cols, entries in pieces:
+                fetch_exp(ea4[:, t, cols], t, n4_list[:, entries], 3, bias2[:, t, 1:2])
+                nc.vector.scalar_tensor_tensor(
+                    result[:, t, cols], ea4[:, t, cols], -3.0, triple[:, t, cols], ALU.mult, ALU.add
+                )
+                nc.sync.dma_start(out_rows[:, t, cols], result[:, t, cols])

@@ -44,7 +44,7 @@ def tile_picked_codeeosetw_none_p_kernel(
         x_bytes = keep.tile([P, T], U8, name="x_bytes", align_bytes=64)
         nc.gpsimd.memset(d_bytes[:, 0 : G // 2].bitcast(I32), 0)
         nc.vector.memset(d_bytes[:, G // 2 : G].bitcast(I32), 0)
-        nc.gpsimd.memset(x_bytes[:].bitcast(I32), 0)
+        nc.vector.memset(x_bytes[:].bitcast(I32), 0)
 
         k1_list = load_list("k1_list", k1)
         offs_list = load_list("offs_list", offs)
@@ -52,154 +52,194 @@ def tile_picked_codeeosetw_none_p_kernel(
         nc.sync.dma_start(x_bytes[0:P:8, :].bitcast(I32), x_scales[0].bitcast(I32))
         n2_list = load_list("n2_list", n2)
         n1_list = load_list("n1_list", n1)
+        k2_list = load_list("k2_list", k2)
         d_table = keep.tile([P, G], I32, name="d_table", align_bytes=64)
         nc.sync.dma_start(d_table[:], d_words[0].rearrange("p n t -> p (n t)").bitcast(I32))
         x_table = keep.tile([P, T], I32, name="x_table", align_bytes=64)
         nc.sync.dma_start(x_table[:], x_words[0].rearrange("p n t -> p (n t)").bitcast(I32))
-        k2_list = load_list("k2_list", k2)
         n3_list = load_list("n3_list", n3)
         n4_list = load_list("n4_list", n4)
 
         windows = [keep.tile([P, WINDOW], F32, name="window%d" % t) for t in range(PACK)]
-        for t in range(PACK):
-            nc.vector.memset(windows[t][:, S:WINDOW], 0.0)
+        nc.vector.memset(windows[0][:, S:WINDOW], 0.0)
         quarter = keep.tile([P, 1], F32, name="quarter")
         nc.gpsimd.memset(quarter[:], 0.25)
-        rates = keep.tile([P, 4, 8], F32, name="rates")
+        rates1 = keep.tile([P, 2, 8], F32, name="rates1")
+        rates2 = keep.tile([P, 2, 8], F32, name="rates2")
         gain = keep.tile([P, PACK], F32, name="gain")
-        nc.gpsimd.dma_start(rates[:, 0, 0:PACK], by_row(tau))
-        nc.gpsimd.dma_start(rates[:, 1, 0:PACK], by_row(tau2))
+        nc.gpsimd.dma_start(rates1[:, 0, 0:PACK], by_row(tau))
+        nc.gpsimd.dma_start(rates1[:, 1, 0:PACK], by_row(tau2))
         nc.gpsimd.dma_start(gain[:], by_row(gs))
-        nc.gpsimd.dma_start(rates[:, 2, 0:PACK], by_row(tau3))
-        nc.gpsimd.dma_start(rates[:, 3, 0:PACK], by_row(tau4))
+        nc.gpsimd.dma_start(rates2[:, 0, 0:PACK], by_row(tau3))
+        nc.gpsimd.dma_start(rates2[:, 1, 0:PACK], by_row(tau4))
 
-        def pick_scales(name, codes, tag, dealt):
-            picked = keep.tile([P, H], U8, name=name + "_picked_bytes", tag=tag, align_bytes=64)
-            nc.vector.tensor_copy(picked[:], d_bytes[:].indirect(codes[:]))
+        def pick(name, table, places, dtype, tag):
+            picked = keep.tile([P, H], dtype, name=name, tag=tag, align_bytes=64)
+            nc.vector.tensor_copy(picked[:], table.indirect(places[:]))
+            return picked
+
+        def deal(dealt, picked, tiles, run):
             nc.vector.tensor_copy(
-                dealt.rearrange("p (t m) -> p t m", t=PACK), picked[:].rearrange("p (m t) -> p t m", t=PACK)
+                dealt.rearrange("p (t g i) -> p g t i", t=PACK, i=run)[:, :, tiles, :],
+                picked[:].rearrange("p (g i t) -> p g t i", t=PACK, i=run)[:, :, tiles, :],
             )
 
         def place_scales(plane, queues):
             for j, queue in zip(range(1, 4), queues):
                 queue.dma_start(plane[j:P:32, :].bitcast(I32), plane[8 * j : P : 32, :].bitcast(I32))
 
-        def pick_words(name, codes, tag):
-            picked = keep.tile([P, H], U32, name=name + "_picked_words", tag=tag, align_bytes=64)
-            nc.vector.tensor_copy(picked[:], d_table[:].bitcast(U32).indirect(codes[:]))
-            dealt = keep.tile([P, H], U32, name=name + "_words", align_bytes=64)
-            nc.vector.tensor_copy(
-                dealt[:].rearrange("p (t m) -> p t m", t=PACK), picked[:].rearrange("p (m t) -> p t m", t=PACK)
-            )
-            return dealt
-
-        def product(t, cols, w_words, w_bytes, a_words, a_bytes):
+        def product(acc, t, w_words, w_bytes, a_words, a_bytes):
             rows = slice(t * P, (t + 1) * P)
-            bank = psum.tile([P, S], F32, name="bank")
-            acc = bank[:, 0 : cols.stop - cols.start]
             nc.tensor.matmul_mx(
                 out=acc,
                 lhsT=w_words[:, rows].bitcast(FP8X4),
                 lhsT_scale=w_bytes[:, rows],
-                rhs=a_words[:, cols].bitcast(FP8X4),
-                rhs_scale=a_bytes[:, cols],
+                rhs=a_words.bitcast(FP8X4),
+                rhs_scale=a_bytes,
                 start=True,
                 stop=True,
             )
-            return acc
 
-        def layer(name, first_rate, w_words, w_bytes, a_words, a_bytes):
+        def layer(name, rates, order, w_words, w_bytes, a_words, a_bytes):
             tops = keep.tile([P, PACK + 1], F32, name=name + "_tops")
             biases = keep.tile([P, PACK, 2], F32, name=name + "_biases")
+
+            def empty(t, cols, acc, so_far, top):
+                nc.vector.tensor_scalar(windows[t][:, cols], acc, 0.0625, so_far, ALU.mult, ALU.max, accum_out=top)
+
             for t in range(PACK):
-                pieces = halves if t == 0 else [slice(0, S)]
-                so_far = None
-                for i, cols in enumerate(pieces):
-                    acc = product(t, cols, w_words, w_bytes, a_words, a_bytes)
-                    last = i == len(pieces) - 1
-                    top = tops[:, t : t + 1] if last else tops[:, PACK : PACK + 1]
-                    nc.vector.tensor_scalar(
-                        windows[t][:, cols], acc, 0.0625, so_far, ALU.mult, ALU.max, accum_out=top
-                    )
-                    so_far = top
+                top = tops[:, t : t + 1]
+                if t == 0:
+                    first_top = tops[:, PACK : PACK + 1]
+                    for i, so_far, now in ((order[0], None, first_top), (order[1], first_top, top)):
+                        bank = psum.tile([P, S], F32, name="bank")
+                        product(bank[:, 0:HALF], t, w_words, w_bytes, a_words[i], a_bytes[i])
+                        empty(t, halves[i], bank[:, 0:HALF], so_far, now)
+                else:
+                    bank = psum.tile([P, S], F32, name="bank")
+                    for i in order:
+                        product(bank[:, halves[i]], t, w_words, w_bytes, a_words[i], a_bytes[i])
+                    empty(t, slice(0, S), bank[:], None, top)
                 nc.vector.tensor_scalar(
-                    biases[:, t, :], rates[:, first_rate : first_rate + 2, t], so_far, -1.0, ALU.mult, ALU.mult
+                    biases[:, t, :], rates[:, :, t], top, -1.0, ALU.mult, ALU.mult
                 )
             return biases
 
-        def fetch_exp(dst, t, places, rate, bias):
+        def fetch_exp(dst, t, places, rates, biases, which):
             nc.scalar.activation(
-                dst, windows[t][:].indirect(places), ACT.Exp, bias=bias, scale=rates[:, rate, t : t + 1]
+                dst,
+                windows[t][:].indirect(places),
+                ACT.Exp,
+                bias=biases[:, t, which : which + 1],
+                scale=rates[:, which, t : t + 1],
             )
 
+        d_codes = d_table[:].bitcast(U32)
+        x_codes = x_table[:].bitcast(U32)
         plane1 = keep.tile([P, H + S], U8, name="plane1", tag="plane1", align_bytes=64)
         w1_bytes, xq_bytes = plane1[:, 0:H], plane1[:, H : H + S]
-        pick_scales("w1", k1_list, "w1_picked_bytes", w1_bytes)
-        x_picked_bytes = keep.tile([P, S], U8, name="x_picked_bytes", align_bytes=64)
-        nc.vector.tensor_copy(x_picked_bytes[:], x_bytes[:].indirect(offs_list[:]))
+        w1_picked_bytes = pick("w1_picked_bytes", d_bytes[:], k1_list, U8, "w1_picked_bytes")
+        x_picked_bytes = pick("x_picked_bytes", x_bytes[:], offs_list, U8, "x_picked_bytes")
+        deal(w1_bytes, w1_picked_bytes, slice(0, PACK), 16)
         nc.vector.tensor_copy(xq_bytes.bitcast(I32), x_picked_bytes[:].bitcast(I32))
         place_scales(plane1, [nc.scalar, nc.sync, nc.scalar])
-        w1_words = pick_words("w1", k1_list, "w1_picked_words")
-        xq_words = keep.tile([P, S], U32, name="xq_words", tag="xq_words", align_bytes=64)
-        for cols, entries in zip(halves, list_halves):
-            nc.vector.tensor_copy(xq_words[:, cols], x_table[:].bitcast(U32).indirect(offs_list[:, entries]))
+        w1_picked_words = pick("w1_picked_words", d_codes, k1_list, U32, "w1_picked_words")
+        w1_words = keep.tile([P, H], U32, name="w1_words", align_bytes=64)
+        xq_first = keep.tile([P, HALF], U32, name="xq_first", align_bytes=64)
+        xq_second = keep.tile([P, HALF], U32, name="xq_second", tag="xq_words", align_bytes=64)
+        xq_words = [xq_first[:], xq_second[:]]
+        nc.vector.tensor_copy(xq_words[0], x_codes.indirect(offs_list[:, list_halves[0]]))
+        deal(w1_words[:], w1_picked_words, slice(0, 1), 4)
+        nc.vector.tensor_copy(xq_words[1], x_codes.indirect(offs_list[:, list_halves[1]]))
+        deal(w1_words[:], w1_picked_words, slice(1, PACK), 4)
 
-        bias1 = layer("h", 0, w1_words, w1_bytes, xq_words, xq_bytes)
+        bias1 = layer("h", rates1, (0, 1), w1_words, w1_bytes, xq_words, [xq_bytes[:, cols] for cols in halves])
         ea = keep.tile([P, PACK, S], F32, name="ea")
-        ea2 = keep.tile([P, PACK, S], F32, name="ea2")
+        last_ea2 = keep.tile([P, S], F32, name="last_ea2")
+        ea2 = [windows[t + 1][:, S:WINDOW] for t in range(PACK - 1)] + [last_ea2[:]]
         for t in range(PACK):
-            fetch_exp(ea2[:, t, :], t, n2_list[:], 1, bias1[:, t, 1:2])
-            fetch_exp(ea[:, t, :], t, n1_list[:], 0, bias1[:, t, 0:1])
+            fetch_exp(ea2[t], t, n2_list[:], rates1, bias1, 1)
+            fetch_exp(ea[:, t, :], t, n1_list[:], rates1, bias1, 0)
 
         w2_bytes = keep.tile([P, H], U8, name="w2_bytes", align_bytes=64)
-        pick_scales("w2", k2_list, "plane1", w2_bytes[:])
+        w2_words = keep.tile([P, H], U32, name="w2_words", align_bytes=64)
+        w2_picked_bytes = pick("w2_picked_bytes", d_bytes[:], k2_list, U8, "plane1")
+        w2_picked_words = pick("w2_picked_words", d_codes, k2_list, U32, "xq_words")
+        deal(w2_bytes[:], w2_picked_bytes, slice(0, PACK), 16)
         place_scales(w2_bytes, [nc.sync] * 3)
-        w2_words = pick_words("w2", k2_list, "xq_words")
+        deal(w2_words[:], w2_picked_words, slice(0, PACK), 4)
+
+        den1 = keep.tile([P, S], F32, name="den1", tag="xq_words", align_bytes=64)
+        pairs = keep.tile([P, S], F32, name="pairs")
+        fours = keep.tile([P, HALF], F32, name="fours")
+        inv_fours = keep.tile([P, HALF], F32, name="inv_fours")
+        inv_pairs = keep.tile([P, S], F32, name="inv_pairs")
+        inv_den = keep.tile([P, 2, S], F32, name="inv_den", tag="inv_den")
+        quotient = keep.tile([P, 2, S], F32, name="quotient")
+        nc.vector.tensor_scalar(den1[:], ea2[1], 0.25, None, ALU.add)
+        nc.vector.scalar_tensor_tensor(pairs[:], ea2[0], 0.25, den1[:], ALU.add, ALU.mult)
+        nc.vector.tensor_tensor(fours[:], pairs[:, halves[0]], pairs[:, halves[1]], ALU.mult)
+        nc.vector.reciprocal(inv_fours[:], fours[:])
+        for i in range(2):
+            nc.vector.tensor_tensor(inv_pairs[:, halves[i]], inv_fours[:], pairs[:, halves[1 - i]], ALU.mult)
+        nc.vector.tensor_tensor(inv_den[:, 0, :], inv_pairs[:], den1[:], ALU.mult)
+        nc.vector.scalar_tensor_tensor(inv_den[:, 1, :], ea2[0], 0.25, inv_pairs[:], ALU.add, ALU.mult)
+        for t in range(2):
+            nc.vector.scalar_tensor_tensor(quotient[:, t, :], ea[:, t, :], 0.25, inv_den[:, t, :], ALU.add, ALU.mult)
+
         half_h = keep.tile([P, PACK, S], F32, name="half_h")
         for t in range(PACK):
             nc.vector.tensor_scalar(
                 half_h[:, t, :], windows[t][:, 0:S], gain[:, t : t + 1], 0.5, ALU.mult, ALU.mult
             )
 
-        log_den = keep.tile([P, PACK, S], F32, name="log_den")
+        log_den = keep.tile([P, 2, S], F32, name="log_den")
         log_num = keep.tile([P, PACK, S], F32, name="log_num")
-        rest = keep.tile([P, PACK, S], F32, name="rest")
+        rest = keep.tile([P, 2, S], F32, name="rest", tag="inv_den")
         z_rows = keep.tile([P, PACK, S], BF16, name="z_rows")
-        z_packed = keep.tile([P, S, PACK], BF16, name="z_packed", align_bytes=64)
-        z_words = keep.tile([P, S], U32, name="z_words", align_bytes=64)
-        z_bytes = keep.tile([P, S], U8, name="z_bytes", align_bytes=64)
-        for t in range(PACK):
-            nc.scalar.activation(log_den[:, t, :], ea2[:, t, :], ACT.Ln, bias=quarter[:], scale=1.0)
+        z_packed = [keep.tile([P, HALF, PACK], BF16, name="z_packed%d" % i, align_bytes=64) for i in range(2)]
+        z_words = [keep.tile([P, HALF], U32, name="z_words%d" % i, align_bytes=64) for i in range(2)]
+        z_bytes = [keep.tile([P, HALF], U8, name="z_bytes%d" % i, align_bytes=64) for i in range(2)]
+        for t in (3, 2):
+            nc.scalar.activation(log_den[:, t - 2, :], ea2[t], ACT.Ln, bias=quarter[:], scale=1.0)
             nc.vector.scalar_tensor_tensor(
-                rest[:, t, :], log_den[:, t, :], gain[:, t : t + 1], half_h[:, t, :], ALU.mult, ALU.subtract
+                rest[:, t - 2, :], log_den[:, t - 2, :], gain[:, t : t + 1], half_h[:, t, :], ALU.mult, ALU.subtract
             )
         for cols in halves:
-            for t in range(PACK):
+            for t in (3, 2):
                 nc.scalar.activation(log_num[:, t, cols], ea[:, t, cols], ACT.Ln, bias=quarter[:], scale=1.0)
                 nc.vector.scalar_tensor_tensor(
-                    z_rows[:, t, cols], log_num[:, t, cols], gain[:, t : t + 1], rest[:, t, cols], ALU.mult, ALU.subtract
+                    z_rows[:, t, cols], log_num[:, t, cols], gain[:, t : t + 1], rest[:, t - 2, cols], ALU.mult, ALU.subtract
                 )
-            nc.vector.tensor_copy(
-                z_packed[:, cols, :], z_rows[:, :, cols].rearrange("p t c -> p c t")
+            for t in (0, 1):
+                nc.scalar.activation(log_num[:, t, cols], quotient[:, t, cols], ACT.Ln)
+                nc.vector.scalar_tensor_tensor(
+                    z_rows[:, t, cols], log_num[:, t, cols], gain[:, t : t + 1], half_h[:, t, cols], ALU.mult, ALU.add
+                )
+        for i, copy in enumerate((nc.scalar.copy, nc.vector.tensor_copy)):
+            copy(
+                z_packed[i][:].rearrange("p (c i) t -> p c t i", i=4),
+                z_rows[:, :, halves[i]].rearrange("p t (c i) -> p c t i", i=4),
             )
+        for i in (1, 0):
             nc.vector.quantize_mx(
-                out=z_words[:, cols].bitcast(FP8X4),
-                scales=z_bytes[:, cols],
-                in_=z_packed[:, cols, :].rearrange("p c t -> p (c t)"),
+                out=z_words[i][:].bitcast(FP8X4),
+                scales=z_bytes[i][:],
+                in_=z_packed[i][:].rearrange("p c t -> p (c t)"),
             )
 
-        bias2 = layer("h2", 2, w2_words, w2_bytes, z_words, z_bytes)
+        bias2 = layer("h2", rates2, (1, 0), w2_words, w2_bytes, [w[:] for w in z_words], [b[:] for b in z_bytes])
         ea3 = keep.tile([P, PACK, S], F32, name="ea3")
         ea4 = keep.tile([P, PACK, S], F32, name="ea4")
         triple = keep.tile([P, PACK, S], F32, name="triple")
         result = keep.tile([P, PACK, S], F32, name="result")
         out_rows = out.rearrange("(p t) n -> p t n", t=PACK)
         for t in range(PACK):
-            fetch_exp(ea3[:, t, :], t, n3_list[:], 2, bias2[:, t, 0:1])
+            fetch_exp(ea3[:, t, :], t, n3_list[:], rates2, bias2, 0)
             nc.vector.tensor_scalar(triple[:, t, :], ea3[:, t, :], 3.0, None, ALU.mult)
             pieces = zip(halves, list_halves) if t == PACK - 1 else [(slice(0, S), slice(0, LIST_COLS))]
             for cols, entries in pieces:
-                fetch_exp(ea4[:, t, cols], t, n4_list[:, entries], 3, bias2[:, t, 1:2])
+                fetch_exp(ea4[:, t, cols], t, n4_list[:, entries], rates2, bias2, 1)
                 nc.vector.scalar_tensor_tensor(
                     result[:, t, cols], ea4[:, t, cols], -3.0, triple[:, t, cols], ALU.mult, ALU.add
                 )

@@ -88,42 +88,42 @@ def tile_picked_codeeosetw_none_p_kernel(
             for j, queue in zip(range(1, 4), queues):
                 queue.dma_start(plane[j:P:32, :].bitcast(I32), plane[8 * j : P : 32, :].bitcast(I32))
 
-        def product(acc, t, w_words, w_bytes, a_words, a_bytes):
-            rows = slice(t * P, (t + 1) * P)
+        def product(acc, w_words, w_bytes, a_words, a_bytes):
             nc.tensor.matmul_mx(
                 out=acc,
-                lhsT=w_words[:, rows].bitcast(FP8X4),
-                lhsT_scale=w_bytes[:, rows],
+                lhsT=w_words.bitcast(FP8X4),
+                lhsT_scale=w_bytes,
                 rhs=a_words.bitcast(FP8X4),
                 rhs_scale=a_bytes,
                 start=True,
                 stop=True,
             )
 
-        def layer(name, rates, order, w_words, w_bytes, a_words, a_bytes):
-            tops = keep.tile([P, PACK + 1], F32, name=name + "_tops")
-            biases = keep.tile([P, PACK, 2], F32, name=name + "_biases")
+        def empty(t, cols, acc, so_far, top):
+            nc.vector.tensor_scalar(windows[t][:, cols], acc, 0.0625, so_far, ALU.mult, ALU.max, accum_out=top)
 
-            def empty(t, cols, acc, so_far, top):
-                nc.vector.tensor_scalar(windows[t][:, cols], acc, 0.0625, so_far, ALU.mult, ALU.max, accum_out=top)
+        def bias_of(t, biases, rates, top):
+            nc.vector.tensor_scalar(biases[:, t, :], rates[:, :, t], top, -1.0, ALU.mult, ALU.mult)
 
-            for t in range(PACK):
-                top = tops[:, t : t + 1]
-                if t == 0:
-                    first_top = tops[:, PACK : PACK + 1]
-                    for i, so_far, now in ((order[0], None, first_top), (order[1], first_top, top)):
-                        bank = psum.tile([P, S], F32, name="bank")
-                        product(bank[:, 0:HALF], t, w_words, w_bytes, a_words[i], a_bytes[i])
-                        empty(t, halves[i], bank[:, 0:HALF], so_far, now)
-                else:
-                    bank = psum.tile([P, S], F32, name="bank")
-                    for i in order:
-                        product(bank[:, halves[i]], t, w_words, w_bytes, a_words[i], a_bytes[i])
-                    empty(t, slice(0, S), bank[:], None, top)
-                nc.vector.tensor_scalar(
-                    biases[:, t, :], rates[:, :, t], top, -1.0, ALU.mult, ALU.mult
-                )
-            return biases
+        def first_tile(name, biases, rates, order, w_words, w_bytes, a_words, a_bytes):
+            half_top = keep.tile([P, 1], F32, name=name + "_half_top", tag=name + "_half_top", align_bytes=64)
+            top = keep.tile([P, 1], F32, name="top", tag="top")
+            for i, so_far, now in ((order[0], None, half_top[:]), (order[1], half_top[:], top[:])):
+                bank = psum.tile([P, S], F32, name="bank")
+                product(bank[:, 0:HALF], w_words, w_bytes, a_words[i], a_bytes[i])
+                empty(0, halves[i], bank[:, 0:HALF], so_far, now)
+            bias_of(0, biases, rates, top[:])
+
+        def later_tile(t, biases, rates, w_words, w_bytes, a_words, a_bytes):
+            bank = psum.tile([P, S], F32, name="bank")
+            for i in range(2):
+                product(bank[:, halves[i]], w_words, w_bytes, a_words[i], a_bytes[i])
+            top = keep.tile([P, 1], F32, name="top", tag="top")
+            empty(t, slice(0, S), bank[:], None, top[:])
+            bias_of(t, biases, rates, top[:])
+
+        def rows_of(t):
+            return slice(t * P, (t + 1) * P)
 
         def fetch_exp(dst, t, places, rates, biases, which):
             nc.scalar.activation(
@@ -144,16 +144,21 @@ def tile_picked_codeeosetw_none_p_kernel(
         nc.vector.tensor_copy(xq_bytes.bitcast(I32), x_picked_bytes[:].bitcast(I32))
         place_scales(plane1, [nc.scalar, nc.sync, nc.scalar])
         w1_picked_words = pick("w1_picked_words", d_codes, k1_list, U32, "w1_picked_words")
-        w1_words = keep.tile([P, H], U32, name="w1_words", align_bytes=64)
+        w1_first = keep.tile([P, P], U32, name="w1_first", align_bytes=64)
         xq_first = keep.tile([P, HALF], U32, name="xq_first", align_bytes=64)
         xq_second = keep.tile([P, HALF], U32, name="xq_second", tag="xq_words", align_bytes=64)
         xq_words = [xq_first[:], xq_second[:]]
         nc.vector.tensor_copy(xq_words[0], x_codes.indirect(offs_list[:, list_halves[0]]))
-        deal(w1_words[:], w1_picked_words, slice(0, 1), 4)
+        nc.vector.tensor_copy(w1_first[:], w1_picked_words[:, 0:H:PACK])
         nc.vector.tensor_copy(xq_words[1], x_codes.indirect(offs_list[:, list_halves[1]]))
-        deal(w1_words[:], w1_picked_words, slice(1, PACK), 4)
+        xq_scales = [xq_bytes[:, cols] for cols in halves]
+        bias1 = keep.tile([P, PACK, 2], F32, name="bias1")
+        first_tile("h", bias1, rates1, (0, 1), w1_first[:], w1_bytes[:, rows_of(0)], xq_words, xq_scales)
+        w1_later = keep.tile([P, H], U32, name="w1_later", tag="h_half_top", align_bytes=64)
+        deal(w1_later[:], w1_picked_words, slice(1, PACK), 4)
+        for t in range(1, PACK):
+            later_tile(t, bias1, rates1, w1_later[:, rows_of(t)], w1_bytes[:, rows_of(t)], xq_words, xq_scales)
 
-        bias1 = layer("h", rates1, (0, 1), w1_words, w1_bytes, xq_words, [xq_bytes[:, cols] for cols in halves])
         ea = keep.tile([P, PACK, S], F32, name="ea")
         last_ea2 = keep.tile([P, S], F32, name="last_ea2")
         ea2 = [windows[t + 1][:, S:WINDOW] for t in range(PACK - 1)] + [last_ea2[:]]
@@ -169,66 +174,64 @@ def tile_picked_codeeosetw_none_p_kernel(
         place_scales(w2_bytes, [nc.sync] * 3)
         deal(w2_words[:], w2_picked_words, slice(0, PACK), 4)
 
-        den1 = keep.tile([P, S], F32, name="den1", tag="xq_words", align_bytes=64)
-        pairs = keep.tile([P, S], F32, name="pairs")
-        fours = keep.tile([P, HALF], F32, name="fours")
-        inv_fours = keep.tile([P, HALF], F32, name="inv_fours")
-        inv_pairs = keep.tile([P, S], F32, name="inv_pairs")
-        inv_den = keep.tile([P, 2, S], F32, name="inv_den", tag="inv_den")
-        quotient = keep.tile([P, 2, S], F32, name="quotient")
-        nc.vector.tensor_scalar(den1[:], ea2[1], 0.25, None, ALU.add)
-        nc.vector.scalar_tensor_tensor(pairs[:], ea2[0], 0.25, den1[:], ALU.add, ALU.mult)
-        nc.vector.tensor_tensor(fours[:], pairs[:, halves[0]], pairs[:, halves[1]], ALU.mult)
-        nc.vector.reciprocal(inv_fours[:], fours[:])
+        den = keep.tile([P, S], F32, name="den", tag="xq_words", align_bytes=64)
+        pairs = keep.tile([P, HALF], F32, name="pairs")
+        inv_pairs = keep.tile([P, HALF], F32, name="inv_pairs")
+        inv_den = keep.tile([P, S], F32, name="inv_den", tag="inv_den")
+        quotient = keep.tile([P, S], F32, name="quotient")
+        nc.vector.tensor_scalar(den[:], ea2[0], 0.25, None, ALU.add)
+        nc.vector.tensor_tensor(pairs[:], den[:, halves[0]], den[:, halves[1]], ALU.mult)
+        nc.vector.reciprocal(inv_pairs[:], pairs[:])
         for i in range(2):
-            nc.vector.tensor_tensor(inv_pairs[:, halves[i]], inv_fours[:], pairs[:, halves[1 - i]], ALU.mult)
-        nc.vector.tensor_tensor(inv_den[:, 0, :], inv_pairs[:], den1[:], ALU.mult)
-        nc.vector.scalar_tensor_tensor(inv_den[:, 1, :], ea2[0], 0.25, inv_pairs[:], ALU.add, ALU.mult)
-        for t in range(2):
-            nc.vector.scalar_tensor_tensor(quotient[:, t, :], ea[:, t, :], 0.25, inv_den[:, t, :], ALU.add, ALU.mult)
+            nc.vector.tensor_tensor(inv_den[:, halves[i]], inv_pairs[:], den[:, halves[1 - i]], ALU.mult)
+        nc.vector.scalar_tensor_tensor(quotient[:], ea[:, 0, :], 0.25, inv_den[:], ALU.add, ALU.mult)
 
         half_h = keep.tile([P, PACK, S], F32, name="half_h")
         for t in range(PACK):
-            nc.vector.tensor_scalar(
+            nc.gpsimd.tensor_scalar(
                 half_h[:, t, :], windows[t][:, 0:S], gain[:, t : t + 1], 0.5, ALU.mult, ALU.mult
             )
 
-        log_den = keep.tile([P, 2, S], F32, name="log_den")
-        log_num = keep.tile([P, PACK, S], F32, name="log_num")
-        rest = keep.tile([P, 2, S], F32, name="rest", tag="inv_den")
+        logs = keep.tile([P, 2, PACK, S], F32, name="logs", tag="inv_den")
+        log_num, log_den = logs[:, 0], logs[:, 1]
+        rest = keep.tile([P, PACK, S], F32, name="rest")
         z_rows = keep.tile([P, PACK, S], BF16, name="z_rows")
         z_packed = [keep.tile([P, HALF, PACK], BF16, name="z_packed%d" % i, align_bytes=64) for i in range(2)]
         z_words = [keep.tile([P, HALF], U32, name="z_words%d" % i, align_bytes=64) for i in range(2)]
         z_bytes = [keep.tile([P, HALF], U8, name="z_bytes%d" % i, align_bytes=64) for i in range(2)]
-        for t in (3, 2):
-            nc.scalar.activation(log_den[:, t - 2, :], ea2[t], ACT.Ln, bias=quarter[:], scale=1.0)
+        nc.scalar.activation(log_num[:, 0, :], quotient[:], ACT.Ln)
+        nc.vector.scalar_tensor_tensor(
+            z_rows[:, 0, :], log_num[:, 0, :], gain[:, 0:1], half_h[:, 0, :], ALU.mult, ALU.add
+        )
+        for t in range(1, PACK):
+            nc.scalar.activation(log_den[:, t, :], ea2[t], ACT.Ln, bias=quarter[:], scale=1.0)
             nc.vector.scalar_tensor_tensor(
-                rest[:, t - 2, :], log_den[:, t - 2, :], gain[:, t : t + 1], half_h[:, t, :], ALU.mult, ALU.subtract
+                rest[:, t, :], log_den[:, t, :], gain[:, t : t + 1], half_h[:, t, :], ALU.mult, ALU.subtract
             )
         for cols in halves:
-            for t in (3, 2):
+            for t in range(1, PACK):
                 nc.scalar.activation(log_num[:, t, cols], ea[:, t, cols], ACT.Ln, bias=quarter[:], scale=1.0)
                 nc.vector.scalar_tensor_tensor(
-                    z_rows[:, t, cols], log_num[:, t, cols], gain[:, t : t + 1], rest[:, t - 2, cols], ALU.mult, ALU.subtract
-                )
-            for t in (0, 1):
-                nc.scalar.activation(log_num[:, t, cols], quotient[:, t, cols], ACT.Ln)
-                nc.vector.scalar_tensor_tensor(
-                    z_rows[:, t, cols], log_num[:, t, cols], gain[:, t : t + 1], half_h[:, t, cols], ALU.mult, ALU.add
+                    z_rows[:, t, cols], log_num[:, t, cols], gain[:, t : t + 1], rest[:, t, cols], ALU.mult, ALU.subtract
                 )
         for i, copy in enumerate((nc.scalar.copy, nc.vector.tensor_copy)):
             copy(
                 z_packed[i][:].rearrange("p (c i) t -> p c t i", i=4),
                 z_rows[:, :, halves[i]].rearrange("p t (c i) -> p c t i", i=4),
             )
-        for i in (1, 0):
+        for i in range(2):
             nc.vector.quantize_mx(
                 out=z_words[i][:].bitcast(FP8X4),
                 scales=z_bytes[i][:],
                 in_=z_packed[i][:].rearrange("p c t -> p (c t)"),
             )
 
-        bias2 = layer("h2", rates2, (1, 0), w2_words, w2_bytes, [w[:] for w in z_words], [b[:] for b in z_bytes])
+        zq_words = [w[:] for w in z_words]
+        zq_scales = [b[:] for b in z_bytes]
+        bias2 = keep.tile([P, PACK, 2], F32, name="bias2")
+        first_tile("h2", bias2, rates2, (0, 1), w2_words[:, rows_of(0)], w2_bytes[:, rows_of(0)], zq_words, zq_scales)
+        for t in range(1, PACK):
+            later_tile(t, bias2, rates2, w2_words[:, rows_of(t)], w2_bytes[:, rows_of(t)], zq_words, zq_scales)
         ea3 = keep.tile([P, PACK, S], F32, name="ea3")
         ea4 = keep.tile([P, PACK, S], F32, name="ea4")
         triple = keep.tile([P, PACK, S], F32, name="triple")

@@ -18,6 +18,7 @@ K, T, S, G, H = 512, 1024, 512, 2048, 512
 HALF = S // 2
 WINDOW = 2 * S
 LIST_COLS = S // 16
+LINE = 16
 FLOPS = 2 * 2 * K * H * S
 
 
@@ -39,6 +40,9 @@ def tile_picked_codeeosetw_none_p_kernel(
 
         def by_row(vec):
             return vec.rearrange("(p t) o -> p (t o)", t=PACK)
+
+        def rows_of(t):
+            return slice(t * P, (t + 1) * P)
 
         d_bytes = keep.tile([P, G], U8, name="d_bytes", align_bytes=64)
         x_bytes = keep.tile([P, T], U8, name="x_bytes", align_bytes=64)
@@ -84,9 +88,9 @@ def tile_picked_codeeosetw_none_p_kernel(
                 picked[:].rearrange("p (g i t) -> p g t i", t=PACK, i=run)[:, :, tiles, :],
             )
 
-        def place_scales(plane, queues):
+        def place_scales(scales, queues):
             for j, queue in zip(range(1, 4), queues):
-                queue.dma_start(plane[j:P:32, :].bitcast(I32), plane[8 * j : P : 32, :].bitcast(I32))
+                queue.dma_start(scales[j:P:32, :].bitcast(I32), scales[8 * j : P : 32, :].bitcast(I32))
 
         def product(acc, w_words, w_bytes, a_words, a_bytes):
             nc.tensor.matmul_mx(
@@ -105,10 +109,10 @@ def tile_picked_codeeosetw_none_p_kernel(
         def bias_of(t, biases, rates, top):
             nc.vector.tensor_scalar(biases[:, t, :], rates[:, :, t], top, -1.0, ALU.mult, ALU.mult)
 
-        def first_tile(name, biases, rates, order, w_words, w_bytes, a_words, a_bytes):
+        def first_tile(name, biases, rates, w_words, w_bytes, a_words, a_bytes):
             half_top = keep.tile([P, 1], F32, name=name + "_half_top", tag=name + "_half_top", align_bytes=64)
-            top = keep.tile([P, 1], F32, name="top", tag="top")
-            for i, so_far, now in ((order[0], None, half_top[:]), (order[1], half_top[:], top[:])):
+            top = keep.tile([P, 1], F32, name="top", tag="top", align_bytes=64)
+            for i, so_far, now in ((0, None, half_top[:]), (1, half_top[:], top[:])):
                 bank = psum.tile([P, S], F32, name="bank")
                 product(bank[:, 0:HALF], w_words, w_bytes, a_words[i], a_bytes[i])
                 empty(0, halves[i], bank[:, 0:HALF], so_far, now)
@@ -118,12 +122,9 @@ def tile_picked_codeeosetw_none_p_kernel(
             bank = psum.tile([P, S], F32, name="bank")
             for i in range(2):
                 product(bank[:, halves[i]], w_words, w_bytes, a_words[i], a_bytes[i])
-            top = keep.tile([P, 1], F32, name="top", tag="top")
+            top = keep.tile([P, 1], F32, name="top", tag="top", align_bytes=64)
             empty(t, slice(0, S), bank[:], None, top[:])
             bias_of(t, biases, rates, top[:])
-
-        def rows_of(t):
-            return slice(t * P, (t + 1) * P)
 
         def fetch_exp(dst, t, places, rates, biases, which):
             nc.scalar.activation(
@@ -136,26 +137,26 @@ def tile_picked_codeeosetw_none_p_kernel(
 
         d_codes = d_table[:].bitcast(U32)
         x_codes = x_table[:].bitcast(U32)
-        plane1 = keep.tile([P, H + S], U8, name="plane1", tag="plane1", align_bytes=64)
-        w1_bytes, xq_bytes = plane1[:, 0:H], plane1[:, H : H + S]
+        scales1 = keep.tile([P, H + S], U8, name="scales1", align_bytes=64)
+        w1_bytes, xq_bytes = scales1[:, 0:H], scales1[:, H : H + S]
         w1_picked_bytes = pick("w1_picked_bytes", d_bytes[:], k1_list, U8, "w1_picked_bytes")
         x_picked_bytes = pick("x_picked_bytes", x_bytes[:], offs_list, U8, "x_picked_bytes")
-        deal(w1_bytes, w1_picked_bytes, slice(0, PACK), 16)
+        deal(w1_bytes, w1_picked_bytes, slice(0, PACK), LINE)
         nc.vector.tensor_copy(xq_bytes.bitcast(I32), x_picked_bytes[:].bitcast(I32))
-        place_scales(plane1, [nc.scalar, nc.sync, nc.scalar])
+        place_scales(scales1, [nc.scalar, nc.sync, nc.scalar])
         w1_picked_words = pick("w1_picked_words", d_codes, k1_list, U32, "w1_picked_words")
         w1_first = keep.tile([P, P], U32, name="w1_first", align_bytes=64)
         xq_first = keep.tile([P, HALF], U32, name="xq_first", align_bytes=64)
-        xq_second = keep.tile([P, HALF], U32, name="xq_second", tag="xq_words", align_bytes=64)
+        xq_second = keep.tile([P, HALF], U32, name="xq_second", tag="xq_second", align_bytes=64)
         xq_words = [xq_first[:], xq_second[:]]
         nc.vector.tensor_copy(xq_words[0], x_codes.indirect(offs_list[:, list_halves[0]]))
         nc.vector.tensor_copy(w1_first[:], w1_picked_words[:, 0:H:PACK])
         nc.vector.tensor_copy(xq_words[1], x_codes.indirect(offs_list[:, list_halves[1]]))
         xq_scales = [xq_bytes[:, cols] for cols in halves]
         bias1 = keep.tile([P, PACK, 2], F32, name="bias1")
-        first_tile("h", bias1, rates1, (0, 1), w1_first[:], w1_bytes[:, rows_of(0)], xq_words, xq_scales)
+        first_tile("h", bias1, rates1, w1_first[:], w1_bytes[:, rows_of(0)], xq_words, xq_scales)
         w1_later = keep.tile([P, H], U32, name="w1_later", tag="h_half_top", align_bytes=64)
-        deal(w1_later[:], w1_picked_words, slice(1, PACK), 4)
+        deal(w1_later[:], w1_picked_words, slice(1, PACK), LINE // 4)
         for t in range(1, PACK):
             later_tile(t, bias1, rates1, w1_later[:, rows_of(t)], w1_bytes[:, rows_of(t)], xq_words, xq_scales)
 
@@ -166,15 +167,7 @@ def tile_picked_codeeosetw_none_p_kernel(
             fetch_exp(ea2[t], t, n2_list[:], rates1, bias1, 1)
             fetch_exp(ea[:, t, :], t, n1_list[:], rates1, bias1, 0)
 
-        w2_bytes = keep.tile([P, H], U8, name="w2_bytes", align_bytes=64)
-        w2_words = keep.tile([P, H], U32, name="w2_words", align_bytes=64)
-        w2_picked_bytes = pick("w2_picked_bytes", d_bytes[:], k2_list, U8, "plane1")
-        w2_picked_words = pick("w2_picked_words", d_codes, k2_list, U32, "xq_words")
-        deal(w2_bytes[:], w2_picked_bytes, slice(0, PACK), 16)
-        place_scales(w2_bytes, [nc.sync] * 3)
-        deal(w2_words[:], w2_picked_words, slice(0, PACK), 4)
-
-        den = keep.tile([P, S], F32, name="den", tag="xq_words", align_bytes=64)
+        den = keep.tile([P, S], F32, name="den", tag="xq_second", align_bytes=64)
         pairs = keep.tile([P, HALF], F32, name="pairs")
         inv_pairs = keep.tile([P, HALF], F32, name="inv_pairs")
         inv_den = keep.tile([P, S], F32, name="inv_den", tag="inv_den")
@@ -186,11 +179,17 @@ def tile_picked_codeeosetw_none_p_kernel(
             nc.vector.tensor_tensor(inv_den[:, halves[i]], inv_pairs[:], den[:, halves[1 - i]], ALU.mult)
         nc.vector.scalar_tensor_tensor(quotient[:], ea[:, 0, :], 0.25, inv_den[:], ALU.add, ALU.mult)
 
+        w2_bytes = keep.tile([P, H], U8, name="w2_bytes", align_bytes=64)
+        w2_words = keep.tile([P, H], U32, name="w2_words", align_bytes=64)
+        w2_picked_bytes = pick("w2_picked_bytes", d_bytes[:], k2_list, U8, "top")
+        deal(w2_bytes[:], w2_picked_bytes, slice(0, PACK), LINE)
+        place_scales(w2_bytes, [nc.sync] * 3)
+        w2_picked_words = pick("w2_picked_words", d_codes, k2_list, U32, "top")
+        deal(w2_words[:], w2_picked_words, slice(0, PACK), LINE // 4)
+
         half_h = keep.tile([P, PACK, S], F32, name="half_h")
         for t in range(PACK):
-            nc.gpsimd.tensor_scalar(
-                half_h[:, t, :], windows[t][:, 0:S], gain[:, t : t + 1], 0.5, ALU.mult, ALU.mult
-            )
+            nc.gpsimd.tensor_scalar(half_h[:, t, :], windows[t][:, 0:S], gain[:, t : t + 1], 0.5, ALU.mult, ALU.mult)
 
         logs = keep.tile([P, 2, PACK, S], F32, name="logs", tag="inv_den")
         log_num, log_den = logs[:, 0], logs[:, 1]
@@ -229,7 +228,7 @@ def tile_picked_codeeosetw_none_p_kernel(
         zq_words = [w[:] for w in z_words]
         zq_scales = [b[:] for b in z_bytes]
         bias2 = keep.tile([P, PACK, 2], F32, name="bias2")
-        first_tile("h2", bias2, rates2, (0, 1), w2_words[:, rows_of(0)], w2_bytes[:, rows_of(0)], zq_words, zq_scales)
+        first_tile("h2", bias2, rates2, w2_words[:, rows_of(0)], w2_bytes[:, rows_of(0)], zq_words, zq_scales)
         for t in range(1, PACK):
             later_tile(t, bias2, rates2, w2_words[:, rows_of(t)], w2_bytes[:, rows_of(t)], zq_words, zq_scales)
         ea3 = keep.tile([P, PACK, S], F32, name="ea3")

from contextlib import ExitStack

import concourse.mybir as mybir

F32 = mybir.dt.float32
BF16 = mybir.dt.bfloat16
I32 = mybir.dt.int32
U32 = mybir.dt.uint32
U16 = mybir.dt.uint16
U8 = mybir.dt.uint8
FP8X4 = mybir.dt.float8_e4m3fn_x4
ALU = mybir.AluOpType
ACT = mybir.ActivationFunctionType

P = 128
PACK = 4
K, T, S, G, H = 512, 1024, 512, 2048, 512
HALF = S // 2
WINDOW = 2 * S
LIST_COLS = S // 16
LINE = 16
FLOPS = 2 * 2 * K * H * S


def tile_picked_codeeosetw_none_p_kernel(
    tc, x_words, x_scales, d_words, d_scales, tau, tau2, gs, tau3, tau4, offs, k1, n1, n2, k2, n3, n4, out
):
    nc = tc.nc
    halves = [slice(0, HALF), slice(HALF, S)]
    list_halves = [slice(0, LIST_COLS // 2), slice(LIST_COLS // 2, LIST_COLS)]

    with ExitStack() as ctx:
        keep = ctx.enter_context(tc.tile_pool(name="keep", bufs=1))
        psum = ctx.enter_context(tc.psum_pool(name="psum", bufs=8))

        def load_list(name, src):
            tile = keep.tile([P, LIST_COLS], U16, name=name)
            nc.sync.dma_start(tile[:], src)
            return tile

        def by_row(vec):
            return vec.rearrange("(p t) o -> p (t o)", t=PACK)

        def rows_of(t):
            return slice(t * P, (t + 1) * P)

        d_bytes = keep.tile([P, G], U8, name="d_bytes", align_bytes=64)
        x_bytes = keep.tile([P, T], U8, name="x_bytes", align_bytes=64)
        nc.gpsimd.memset(d_bytes[:, 0 : G // 2].bitcast(I32), 0)
        nc.vector.memset(d_bytes[:, G // 2 : G].bitcast(I32), 0)
        nc.vector.memset(x_bytes[:].bitcast(I32), 0)

        k1_list = load_list("k1_list", k1)
        offs_list = load_list("offs_list", offs)
        nc.sync.dma_start(d_bytes[0:P:8, :].bitcast(I32), d_scales[0].bitcast(I32))
        nc.sync.dma_start(x_bytes[0:P:8, :].bitcast(I32), x_scales[0].bitcast(I32))
        n2_list = load_list("n2_list", n2)
        n1_list = load_list("n1_list", n1)
        k2_list = load_list("k2_list", k2)
        d_table = keep.tile([P, G], I32, name="d_table", align_bytes=64)
        nc.sync.dma_start(d_table[:], d_words[0].rearrange("p n t -> p (n t)").bitcast(I32))
        x_table = keep.tile([P, T], I32, name="x_table", align_bytes=64)
        nc.sync.dma_start(x_table[:], x_words[0].rearrange("p n t -> p (n t)").bitcast(I32))
        n3_list = load_list("n3_list", n3)
        n4_list = load_list("n4_list", n4)

        windows = [keep.tile([P, WINDOW], F32, name="window%d" % t) for t in range(PACK)]
        nc.vector.memset(windows[0][:, S:WINDOW], 0.0)
        quarter = keep.tile([P, 1], F32, name="quarter")
        nc.gpsimd.memset(quarter[:], 0.25)
        rates1 = keep.tile([P, 2, 8], F32, name="rates1")
        rates2 = keep.tile([P, 2, 8], F32, name="rates2")
        gain = keep.tile([P, PACK], F32, name="gain")
        nc.gpsimd.dma_start(rates1[:, 0, 0:PACK], by_row(tau))
        nc.gpsimd.dma_start(rates1[:, 1, 0:PACK], by_row(tau2))
        nc.gpsimd.dma_start(gain[:], by_row(gs))
        nc.gpsimd.dma_start(rates2[:, 0, 0:PACK], by_row(tau3))
        nc.gpsimd.dma_start(rates2[:, 1, 0:PACK], by_row(tau4))

        def pick(name, table, places, dtype, tag):
            picked = keep.tile([P, H], dtype, name=name, tag=tag, align_bytes=64)
            nc.vector.tensor_copy(picked[:], table.indirect(places[:]))
            return picked

        def deal(dealt, picked, tiles, run):
            nc.vector.tensor_copy(
                dealt.rearrange("p (t g i) -> p g t i", t=PACK, i=run)[:, :, tiles, :],
                picked[:].rearrange("p (g i t) -> p g t i", t=PACK, i=run)[:, :, tiles, :],
            )

        def place_scales(scales, queues):
            for j, queue in zip(range(1, 4), queues):
                queue.dma_start(scales[j:P:32, :].bitcast(I32), scales[8 * j : P : 32, :].bitcast(I32))

        def product(acc, w_words, w_bytes, a_words, a_bytes):
            nc.tensor.matmul_mx(
                out=acc,
                lhsT=w_words.bitcast(FP8X4),
                lhsT_scale=w_bytes,
                rhs=a_words.bitcast(FP8X4),
                rhs_scale=a_bytes,
                start=True,
                stop=True,
            )

        def empty(t, cols, acc, so_far, top):
            nc.vector.tensor_scalar(windows[t][:, cols], acc, 0.0625, so_far, ALU.mult, ALU.max, accum_out=top)

        def bias_of(t, biases, rates, top):
            nc.vector.tensor_scalar(biases[:, t, :], rates[:, :, t], top, -1.0, ALU.mult, ALU.mult)

        def first_tile(name, biases, rates, w_words, w_bytes, a_words, a_bytes):
            half_top = keep.tile([P, 1], F32, name=name + "_half_top", tag=name + "_half_top", align_bytes=64)
            top = keep.tile([P, 1], F32, name="top", tag="top", align_bytes=64)
            for i, so_far, now in ((0, None, half_top[:]), (1, half_top[:], top[:])):
                bank = psum.tile([P, S], F32, name="bank")
                product(bank[:, 0:HALF], w_words, w_bytes, a_words[i], a_bytes[i])
                empty(0, halves[i], bank[:, 0:HALF], so_far, now)
            bias_of(0, biases, rates, top[:])

        def later_tile(t, biases, rates, w_words, w_bytes, a_words, a_bytes):
            bank = psum.tile([P, S], F32, name="bank")
            for i in range(2):
                product(bank[:, halves[i]], w_words, w_bytes, a_words[i], a_bytes[i])
            top = keep.tile([P, 1], F32, name="top", tag="top", align_bytes=64)
            empty(t, slice(0, S), bank[:], None, top[:])
            bias_of(t, biases, rates, top[:])

        def fetch_exp(dst, t, places, rates, biases, which):
            nc.scalar.activation(
                dst,
                windows[t][:].indirect(places),
                ACT.Exp,
                bias=biases[:, t, which : which + 1],
                scale=rates[:, which, t : t + 1],
            )

        d_codes = d_table[:].bitcast(U32)
        x_codes = x_table[:].bitcast(U32)
        scales1 = keep.tile([P, H + S], U8, name="scales1", align_bytes=64)
        w1_bytes, xq_bytes = scales1[:, 0:H], scales1[:, H : H + S]
        w1_picked_bytes = pick("w1_picked_bytes", d_bytes[:], k1_list, U8, "w1_picked_bytes")
        x_picked_bytes = pick("x_picked_bytes", x_bytes[:], offs_list, U8, "x_picked_bytes")
        deal(w1_bytes, w1_picked_bytes, slice(0, PACK), LINE)
        nc.vector.tensor_copy(xq_bytes.bitcast(I32), x_picked_bytes[:].bitcast(I32))
        place_scales(scales1, [nc.scalar, nc.sync, nc.scalar])
        w1_picked_words = pick("w1_picked_words", d_codes, k1_list, U32, "w1_picked_words")
        w1_first = keep.tile([P, P], U32, name="w1_first", align_bytes=64)
        xq_first = keep.tile([P, HALF], U32, name="xq_first", align_bytes=64)
        xq_second = keep.tile([P, HALF], U32, name="xq_second", tag="xq_second", align_bytes=64)
        xq_words = [xq_first[:], xq_second[:]]
        nc.vector.tensor_copy(xq_words[0], x_codes.indirect(offs_list[:, list_halves[0]]))
        nc.vector.tensor_copy(w1_first[:], w1_picked_words[:, 0:H:PACK])
        nc.vector.tensor_copy(xq_words[1], x_codes.indirect(offs_list[:, list_halves[1]]))
        xq_scales = [xq_bytes[:, cols] for cols in halves]
        bias1 = keep.tile([P, PACK, 2], F32, name="bias1")
        first_tile("h", bias1, rates1, w1_first[:], w1_bytes[:, rows_of(0)], xq_words, xq_scales)
        w1_later = keep.tile([P, H], U32, name="w1_later", tag="h_half_top", align_bytes=64)
        deal(w1_later[:], w1_picked_words, slice(1, PACK), LINE // 4)
        for t in range(1, PACK):
            later_tile(t, bias1, rates1, w1_later[:, rows_of(t)], w1_bytes[:, rows_of(t)], xq_words, xq_scales)

        ea = keep.tile([P, PACK, S], F32, name="ea")
        last_ea2 = keep.tile([P, S], F32, name="last_ea2")
        ea2 = [windows[t + 1][:, S:WINDOW] for t in range(PACK - 1)] + [last_ea2[:]]
        for t in range(PACK):
            fetch_exp(ea2[t], t, n2_list[:], rates1, bias1, 1)
            fetch_exp(ea[:, t, :], t, n1_list[:], rates1, bias1, 0)

        den = keep.tile([P, S], F32, name="den", tag="xq_second", align_bytes=64)
        pairs = keep.tile([P, HALF], F32, name="pairs")
        inv_pairs = keep.tile([P, HALF], F32, name="inv_pairs")
        inv_den = keep.tile([P, S], F32, name="inv_den", tag="inv_den")
        quotient = keep.tile([P, S], F32, name="quotient")
        nc.vector.tensor_scalar(den[:], ea2[0], 0.25, None, ALU.add)
        nc.vector.tensor_tensor(pairs[:], den[:, halves[0]], den[:, halves[1]], ALU.mult)
        nc.vector.reciprocal(inv_pairs[:], pairs[:])
        for i in range(2):
            nc.vector.tensor_tensor(inv_den[:, halves[i]], inv_pairs[:], den[:, halves[1 - i]], ALU.mult)
        nc.vector.scalar_tensor_tensor(quotient[:], ea[:, 0, :], 0.25, inv_den[:], ALU.add, ALU.mult)

        w2_bytes = keep.tile([P, H], U8, name="w2_bytes", align_bytes=64)
        w2_words = keep.tile([P, H], U32, name="w2_words", align_bytes=64)
        w2_picked_bytes = pick("w2_picked_bytes", d_bytes[:], k2_list, U8, "top")
        deal(w2_bytes[:], w2_picked_bytes, slice(0, PACK), LINE)
        place_scales(w2_bytes, [nc.sync] * 3)
        w2_picked_words = pick("w2_picked_words", d_codes, k2_list, U32, "top")
        deal(w2_words[:], w2_picked_words, slice(0, PACK), LINE // 4)

        half_h = keep.tile([P, PACK, S], F32, name="half_h")
        for t in range(PACK):
            nc.gpsimd.tensor_scalar(half_h[:, t, :], windows[t][:, 0:S], gain[:, t : t + 1], 0.5, ALU.mult, ALU.mult)

        logs = keep.tile([P, 2, PACK, S], F32, name="logs", tag="inv_den")
        log_num, log_den = logs[:, 0], logs[:, 1]
        rest = keep.tile([P, PACK, S], F32, name="rest")
        z_rows = keep.tile([P, PACK, S], BF16, name="z_rows")
        z_packed = [keep.tile([P, HALF, PACK], BF16, name="z_packed%d" % i, align_bytes=64) for i in range(2)]
        z_words = [keep.tile([P, HALF], U32, name="z_words%d" % i, align_bytes=64) for i in range(2)]
        z_bytes = [keep.tile([P, HALF], U8, name="z_bytes%d" % i, align_bytes=64) for i in range(2)]
        nc.scalar.activation(log_num[:, 0, :], quotient[:], ACT.Ln)
        nc.vector.scalar_tensor_tensor(
            z_rows[:, 0, :], log_num[:, 0, :], gain[:, 0:1], half_h[:, 0, :], ALU.mult, ALU.add
        )
        for t in range(1, PACK):
            nc.scalar.activation(log_den[:, t, :], ea2[t], ACT.Ln, bias=quarter[:], scale=1.0)
            nc.vector.scalar_tensor_tensor(
                rest[:, t, :], log_den[:, t, :], gain[:, t : t + 1], half_h[:, t, :], ALU.mult, ALU.subtract
            )
        for cols in halves:
            for t in range(1, PACK):
                nc.scalar.activation(log_num[:, t, cols], ea[:, t, cols], ACT.Ln, bias=quarter[:], scale=1.0)
                nc.vector.scalar_tensor_tensor(
                    z_rows[:, t, cols], log_num[:, t, cols], gain[:, t : t + 1], rest[:, t, cols], ALU.mult, ALU.subtract
                )
        for i, copy in enumerate((nc.scalar.copy, nc.vector.tensor_copy)):
            copy(
                z_packed[i][:].rearrange("p (c i) t -> p c t i", i=4),
                z_rows[:, :, halves[i]].rearrange("p t (c i) -> p c t i", i=4),
            )
        for i in range(2):
            nc.vector.quantize_mx(
                out=z_words[i][:].bitcast(FP8X4),
                scales=z_bytes[i][:],
                in_=z_packed[i][:].rearrange("p c t -> p (c t)"),
            )

        zq_words = [w[:] for w in z_words]
        zq_scales = [b[:] for b in z_bytes]
        bias2 = keep.tile([P, PACK, 2], F32, name="bias2")
        first_tile("h2", bias2, rates2, w2_words[:, rows_of(0)], w2_bytes[:, rows_of(0)], zq_words, zq_scales)
        for t in range(1, PACK):
            later_tile(t, bias2, rates2, w2_words[:, rows_of(t)], w2_bytes[:, rows_of(t)], zq_words, zq_scales)
        ea3 = keep.tile([P, PACK, S], F32, name="ea3")
        ea4 = keep.tile([P, PACK, S], F32, name="ea4")
        triple = keep.tile([P, PACK, S], F32, name="triple")
        result = keep.tile([P, PACK, S], F32, name="result")
        out_rows = out.rearrange("(p t) n -> p t n", t=PACK)
        for t in range(PACK):
            fetch_exp(ea3[:, t, :], t, n3_list[:], rates2, bias2, 0)
            nc.vector.tensor_scalar(triple[:, t, :], ea3[:, t, :], 3.0, None, ALU.mult)
            pieces = zip(halves, list_halves) if t == PACK - 1 else [(slice(0, S), slice(0, LIST_COLS))]
            for cols, entries in pieces:
                fetch_exp(ea4[:, t, cols], t, n4_list[:, entries], rates2, bias2, 1)
                nc.vector.scalar_tensor_tensor(
                    result[:, t, cols], ea4[:, t, cols], -3.0, triple[:, t, cols], ALU.mult, ALU.add
                )
                nc.sync.dma_start(out_rows[:, t, cols], result[:, t, cols])
